import numpy as np
import ml_dtypes


def mxq(x, axis, fmt="e4m3"):
    dtype, down = {"e4m3": (ml_dtypes.float8_e4m3fn, 7), "e5m2": (ml_dtypes.float8_e5m2, 14)}[fmt]
    v = np.moveaxis(np.asarray(x, np.float32).astype(ml_dtypes.bfloat16).astype(np.float64), axis, -1)
    blocks = v.reshape(v.shape[:-1] + (-1, 32))
    amax = np.abs(blocks).max(-1, keepdims=True)
    byte = np.maximum(np.where(amax > 0, np.frexp(amax)[1] - 1 + 127, 0) - down, 1)
    scale = np.exp2(byte - 127.0)
    codes = (blocks / scale).astype(np.float32).astype(dtype).astype(np.float64)
    return np.moveaxis((codes * scale).reshape(v.shape), -1, axis)


WIDE = False


def mx_kscale(k):
    if not WIDE:
        return np.ones(k)
    levels = np.array([10, -10, 5, -5, 0])
    if k % 512:
        return np.exp2(np.random.permutation(np.resize(levels, k // 32))).repeat(32)
    a = np.empty((k // 512, 16))
    for p in range(k // 512):
        a[p, :8] = np.random.permutation(np.resize(levels, 8))
        for g in range(8):
            far = levels[np.abs(levels - a[p, g]) >= 10]
            a[p, g + 8] = far[np.random.randint(len(far))]
    return np.exp2(a.ravel()).repeat(32)


BF16 = ml_dtypes.bfloat16


def bf(x):
    return np.asarray(x, np.float32).astype(BF16)


def f64(x):
    return np.asarray(x).astype(np.float64)

def planes(Y):
    n, m = Y.shape
    b = f64(bf(Y)).reshape(n // 32, 32, m)
    amax = np.abs(b).max(1)
    byte = np.clip(np.where(amax > 0, np.frexp(amax)[1] - 1 + 127 - 7, 1), 1, 254)
    codes = (b * np.exp2(127.0 - byte)[:, None, :]).reshape(n, m).astype(np.float32).astype(ml_dtypes.float8_e4m3fn).view(np.uint8)
    words = codes.reshape(n // 512, 128, 4, m).transpose(0, 1, 3, 2)
    return np.ascontiguousarray(words), np.ascontiguousarray(byte.astype(np.uint8).reshape(n // 512, 16, m))


B, T, D, E = 2, 1024, 512, 512


def squared_relu(a):
    return np.square(np.maximum(a, 0.0))


def silu(a):
    return a / (1.0 + np.exp(-a))


def setup_inputs():
    c, t = mx_kscale(D), mx_kscale(T)
    return {
        "z": bf(np.random.standard_normal((B, T, D))),
        "g1": bf(np.random.standard_normal(D) * c),
        "b1": bf(np.random.standard_normal(D) * 0.5 * c),
        "g2": bf(np.random.standard_normal(D) / c),
        "r": bf(np.random.standard_normal(T) * t),
        "v": bf(np.random.standard_normal((B, T, E)) / t[None, :, None]),
        "u": bf(np.random.standard_normal((B, T, E))),
    }


def core(z, g1, b1, g2, r, v, u):
    z = f64(z)
    q = z * f64(g1)[None, None, :] + f64(b1)[None, None, :]
    k = z * f64(g2)[None, None, :]
    s = (mxq(q, 2, "e4m3") @ mxq(k, 2, "e4m3").transpose(0, 2, 1)) / np.sqrt(D)
    p = f64(r)[None, None, :] * squared_relu(s)
    o = (mxq(p, 2, "e4m3") @ mxq(f64(v), 1, "e4m3")) / np.sqrt(T)
    return silu(f64(u)) * o


def reference(z, g1, b1, g2, r, v, u):
    R_out = core(z, g1, b1, g2, r, v, u)
    words, scales = planes(np.moveaxis(R_out, 1, 0).reshape(1024, -1))
    return R_out, words, scales

@@ -1,0 +1,428 @@
+from contextlib import ExitStack
+
+import concourse.mybir as mybir
+from concourse.masks import make_identity
+
+B, T, D, E = 2, 1024, 512, 512
+FLOPS = 2 * B * T * T * (D + E)
+
+F32 = mybir.dt.float32
+BF16 = mybir.dt.bfloat16
+I32 = mybir.dt.int32
+U32 = mybir.dt.uint32
+U8 = mybir.dt.uint8
+FP8X4 = mybir.dt.float8_e4m3fn_x4
+ACT = mybir.ActivationFunctionType
+ALU = mybir.AluOpType
+
+P = 128
+G = T // 512
+NCH = B * G * 4
+
+
+def tile_mossformersquaredrelugatedattention_x1_kernel(
+    tc, z, g1, b1, g2, r, v, u, out_0, out_1, out_2
+):
+    nc = tc.nc
+    with ExitStack() as ctx:
+        keep = ctx.enter_context(tc.tile_pool(name="keep", bufs=1))
+        work = ctx.enter_context(tc.tile_pool(name="work", bufs=2))
+        psum = ctx.enter_context(tc.psum_pool(name="psum", bufs=2))
+        ctx.enter_context(tc.manual_schedule())
+
+        def kt(shape, dt, name):
+            return keep.tile(shape, dt, name=name, align_bytes=64)
+
+        def wt(shape, dt, name, bufs):
+            return work.tile(shape, dt, name=name, tag=name, bufs=bufs, align_bytes=64)
+
+        def ps(name, bufs):
+            return psum.tile([P, 512], F32, name=name, tag=name, bufs=bufs)
+
+        g2_t = kt([P, 2, 2], BF16, "g2_t")
+        g1_b = kt([P, 4], BF16, "g1_b")
+        b1_b = kt([P, 4], BF16, "b1_b")
+        r_b = kt([P, G, 4], BF16, "r_b")
+        nc.scalar.dma_start(out=g2_t[:], in_=g2.rearrange("(p u e) -> p u e", u=2, e=2))
+        nc.scalar.dma_start(out=g1_b[:], in_=g1.rearrange("(p t) -> p t", t=4))
+        nc.scalar.dma_start(out=b1_b[:], in_=b1.rearrange("(p t) -> p t", t=4))
+        nc.scalar.dma_start(out=r_b[:], in_=r.rearrange("(g p t) -> p g t", g=G, t=4))
+
+        def rows(x, b, g):
+            return x[b, 512 * g : 512 * (g + 1), :].rearrange("(p t) d -> p t d", t=4)
+
+        z_t, v_t, u_t = {}, {}, {}
+
+        def load_z(b):
+            for g in range(G):
+                for h in range(2):
+                    z_t[b, g, h] = kt([P, 2, D], BF16, "z%d%d%d" % (b, g, h))
+                    nc.sync.dma_start(
+                        out=z_t[b, g, h][:], in_=rows(z, b, g)[:, 2 * h : 2 * h + 2, :]
+                    )
+
+        def load_v(b):
+            for g in range(G):
+                v_t[b, g] = kt([P, 4, E], BF16, "v%d%d" % (b, g))
+                nc.sync.dma_start(out=v_t[b, g][:], in_=rows(v, b, g))
+
+        def load_u(b):
+            for g in range(G):
+                u_t[b, g] = kt([P, 4, E], BF16, "u%d%d" % (b, g))
+                nc.sync.dma_start(out=u_t[b, g][:], in_=rows(u, b, g))
+
+        load_z(0)
+        load_v(0)
+        load_z(1)
+        load_u(0)
+        load_v(1)
+        load_u(1)
+
+        warm = kt([P, 1], F32, "warm")
+        warm_o = kt([P, 1], F32, "warm_o")
+        nc.vector.memset(warm[:], 0.0)
+        nc.scalar.activation(out=warm_o[:], in_=warm[:], func=ACT.Silu)
+        ident = kt([P, P], F32, "ident")
+        make_identity(nc, ident[:])
+        g1_f = kt([P, 4], F32, "g1_f")
+        b1_f = kt([P, 4], F32, "b1_f")
+        r_f = kt([P, G * 4], F32, "r_f")
+        nc.vector.tensor_copy(out=g1_f[:], in_=g1_b[:])
+        nc.vector.tensor_copy(out=b1_f[:], in_=b1_b[:])
+        nc.vector.tensor_scalar(
+            out=r_f[:],
+            in0=r_b[:].rearrange("p g t -> p (g t)"),
+            scalar1=1.0 / D,
+            scalar2=None,
+            op0=ALU.mult,
+        )
+
+        kc, ks, qc, qs = {}, {}, {}, {}
+        for b in range(B):
+            kc[b] = kt([P, T], U32, "kc%d" % b)
+            ks[b] = kt([P, T], U8, "ks%d" % b)
+            qc[b] = kt([P, T], U32, "qc%d" % b)
+            qs[b] = kt([P, T], U8, "qs%d" % b)
+        zt, kb, qp, qb = {}, {}, {}, {}
+
+        def transposes(b, g, h, tag, bufs):
+            bank = ps(tag, bufs)
+            zt[b, g, h] = bank
+            words = z_t[b, g, h][:].rearrange("p t d -> p (t d)").bitcast(F32)
+            for s in range(2):
+                for w in range(2):
+                    nc.tensor.transpose(
+                        bank[:, 256 * w + 128 * s : 256 * w + 128 * (s + 1)],
+                        words[:, 256 * s + w : 256 * (s + 1) : 2],
+                        ident[:],
+                    )
+
+        def k_mul(b, g, h):
+            if h == 0:
+                kb[b, g] = wt([P, 512, 4], BF16, "kb", 2)
+            src = zt[b, g, h][:].bitcast(BF16).rearrange("p (u n e) -> p n u e", u=2, e=2)
+            nc.vector.tensor_tensor(
+                out=kb[b, g][:, 256 * h : 256 * (h + 1), :].rearrange(
+                    "p n (u e) -> p n u e", u=2
+                ),
+                in0=src,
+                in1=g2_t[:].unsqueeze(1).to_broadcast([P, 256, 2, 2]),
+                op=ALU.mult,
+            )
+
+        def k_quant(b, g):
+            c = slice(512 * g, 512 * (g + 1))
+            nc.vector.quantize_mx(
+                out=kc[b][:, c].bitcast(FP8X4),
+                scales=ks[b][:, c],
+                in_=kb[b, g][:].rearrange("p n t -> p (n t)"),
+            )
+
+        def q_affine(b, g, h):
+            if h == 0:
+                qp[b, g] = wt([P, 4, 512], BF16, "qp", 2)
+            src = zt[b, g, h][:].bitcast(BF16).rearrange("p (u n e) -> p u n e", u=2, e=2)
+            for t in range(4):
+                nc.scalar.activation(
+                    out=qp[b, g][:, t, 256 * h : 256 * (h + 1)],
+                    in_=src[:, t // 2, :, t % 2],
+                    func=ACT.Identity,
+                    scale=g1_f[:, t : t + 1],
+                    bias=b1_f[:, t : t + 1],
+                )
+
+        def q_weave(b, g, part, nparts, eng):
+            if part == 0:
+                qb[b, g] = wt([P, 512, 4], BF16, "qb", 2)
+            n = 512 // nparts
+            c = slice(n * part, n * (part + 1))
+            weave(eng, qb[b, g][:, c, :], qp[b, g][:, :, c])
+
+        def weave(eng, dst, src):
+            src = src.rearrange("p t n -> p n t")
+            if eng == "V":
+                nc.vector.tensor_copy(out=dst, in_=src)
+            elif eng == "S":
+                nc.scalar.copy(out=dst, in_=src)
+            else:
+                nc.gpsimd.tensor_scalar(
+                    out=dst, in0=src, scalar1=1.0, scalar2=1.0, op0=ALU.mult, op1=ALU.mult
+                )
+
+        def q_quant(b, g, part, nparts):
+            n = 512 // nparts
+            c = slice(512 * g + n * part, 512 * g + n * (part + 1))
+            nc.vector.quantize_mx(
+                out=qc[b][:, c].bitcast(FP8X4),
+                scales=qs[b][:, c],
+                in_=qb[b, g][:, n * part : n * (part + 1), :].rearrange("p n t -> p (n t)"),
+            )
+
+        vc, vs, vb = {}, {}, {}
+        for b in range(B):
+            vc[b] = kt([P, G, E], U32, "vc%d" % b)
+            vs[b] = kt([P, G, E], U8, "vs%d" % b)
+
+        def v_weave(b, g, part, nparts, eng):
+            if part == 0:
+                vb[b, g] = wt([P, E, 4], BF16, "vb", 2)
+            n = E // nparts
+            c = slice(n * part, n * (part + 1))
+            weave(eng, vb[b, g][:, c, :], v_t[b, g][:, :, c])
+
+        def v_quant(b, g):
+            nc.vector.quantize_mx(
+                out=vc[b][:, g, :].bitcast(FP8X4),
+                scales=vs[b][:, g, :],
+                in_=vb[b, g][:].rearrange("p n t -> p (n t)"),
+            )
+
+        sb, wv, pb, pc, psc, ob, sl, R, obf = {}, {}, {}, {}, {}, {}, {}, {}, {}
+
+        def coords(c):
+            return c // (4 * G), (c // 4) % G, c % 4
+
+        def scores(c, jg):
+            b = coords(c)[0]
+            q0 = 128 * (c % (4 * G))
+            bank = ps("s", 4)
+            sb[c, jg] = bank
+            for t in range(4):
+                k0 = 512 * jg + 128 * t
+                nc.tensor.matmul_mx(
+                    out=bank[:, 128 * t : 128 * (t + 1)],
+                    lhsT=kc[b][:, k0 : k0 + 128].bitcast(FP8X4),
+                    lhsT_scale=ks[b][:, k0 : k0 + 128],
+                    rhs=qc[b][:, q0 : q0 + 128].bitcast(FP8X4),
+                    rhs_scale=qs[b][:, q0 : q0 + 128],
+                    start=True,
+                    stop=True,
+                )
+
+        def gain(c, jg):
+            wv[c, jg] = wt([P, 512], F32, "wv", 4)
+            for t in range(4):
+                n = slice(128 * t, 128 * (t + 1))
+                nc.scalar.activation(
+                    out=wv[c, jg][:, n],
+                    in_=sb[c, jg][:, n],
+                    func=ACT.Copy,
+                    scale=r_f[:, 4 * jg + t : 4 * jg + t + 1],
+                )
+
+        def weights(c, jg):
+            if jg == 0:
+                pb[c] = wt([P, G, 128, 4], BF16, "pb", 3)
+            nc.vector.scalar_tensor_tensor(
+                out=pb[c][:, jg, :, :],
+                in0=sb[c, jg][:].rearrange("p (t n) -> p n t", t=4),
+                scalar=0.0,
+                in1=wv[c, jg][:].rearrange("p (t n) -> p n t", t=4),
+                op0=ALU.max,
+                op1=ALU.mult,
+            )
+
+        def p_quant(c):
+            pc[c] = wt([P, G * 128], U32, "pc", 4)
+            psc[c] = wt([P, G * 128], U8, "psc", 4)
+            nc.vector.quantize_mx(
+                out=pc[c][:].bitcast(FP8X4),
+                scales=psc[c][:],
+                in_=pb[c][:].rearrange("p g n t -> p (g n t)"),
+            )
+
+        def attend(c):
+            b = coords(c)[0]
+            ob[c] = ps("o", 2)
+            for jg in range(G):
+                n = slice(128 * jg, 128 * (jg + 1))
+                nc.tensor.matmul_mx(
+                    out=ob[c][:],
+                    lhsT=pc[c][:, n].bitcast(FP8X4),
+                    lhsT_scale=psc[c][:, n],
+                    rhs=vc[b][:, jg, :].bitcast(FP8X4),
+                    rhs_scale=vs[b][:, jg, :],
+                    start=(jg == 0),
+                    stop=(jg == G - 1),
+                )
+
+        def silu(c):
+            b, ig, t = coords(c)
+            sl[c] = wt([P, E], F32, "sl", 4)
+            nc.scalar.activation(out=sl[c][:], in_=u_t[b, ig][:, t, :], func=ACT.Silu)
+
+        def gate(c, e0, e1):
+            b, ig, t = coords(c)
+            k = c // 4
+            if t == 0:
+                R[k] = wt([P, 4, E], F32, "R", 3)
+            nc.vector.scalar_tensor_tensor(
+                out=R[k][:, t, e0:e1],
+                in0=ob[c][:, e0:e1],
+                scalar=1.0 / 32.0,
+                in1=sl[c][:, e0:e1],
+                op0=ALU.mult,
+                op1=ALU.mult,
+            )
+            nc.sync.dma_start(out=rows(out_0, b, ig)[:, t, e0:e1], in_=R[k][:, t, e0:e1])
+
+        def o_weave(k, part, nparts, eng):
+            if k not in obf:
+                obf[k] = wt([P, E, 4], BF16, "obf", 2)
+            n = E // nparts
+            c = slice(n * part, n * (part + 1))
+            weave(eng, obf[k][:, c, :], R[k][:, :, c])
+
+        def o_quant(k, part, nparts):
+            b, ig = k // G, k % G
+            n = E // nparts
+            e0 = n * part
+            oc = wt([P, n], U32, "oc%d" % nparts, 2)
+            osc = wt([P, n], U8, "osc%d" % nparts, 2)
+            nc.vector.quantize_mx(
+                out=oc[:].bitcast(FP8X4),
+                scales=osc[:],
+                in_=obf[k][:, e0 : e0 + n, :].rearrange("p n t -> p (n t)"),
+            )
+            m = slice(E * b + e0, E * b + e0 + n)
+            nc.sync.dma_start(
+                out=out_1[ig, :, m, :].rearrange("p m t -> p (m t)").bitcast(I32),
+                in_=oc[:].bitcast(I32),
+            )
+            for quad in range(4):
+                nc.sync.dma_start(
+                    out=out_2[ig, 4 * quad : 4 * quad + 4, m].bitcast(I32),
+                    in_=osc[32 * quad : 32 * quad + 4, :].bitcast(I32),
+                )
+
+        transposes(0, 0, 0, "z", 2)
+        transposes(0, 0, 1, "z", 2)
+        transposes(0, 1, 0, "s", 4)
+        transposes(0, 1, 1, "s", 4)
+        for part in range(4):
+            v_weave(0, 0, part, 4, "G")
+        k_mul(0, 0, 0)
+        q_affine(0, 0, 0)
+        k_mul(0, 0, 1)
+        q_affine(0, 0, 1)
+        q_weave(0, 0, 0, 2, "V")
+        q_quant(0, 0, 0, 2)
+        k_quant(0, 0)
+        k_mul(0, 1, 0)
+        k_mul(0, 1, 1)
+        scores(0, 0)
+        q_affine(0, 1, 0)
+        gain(0, 0)
+        k_quant(0, 1)
+        scores(0, 1)
+        q_affine(0, 1, 1)
+        gain(0, 1)
+        q_weave(0, 0, 1, 2, "V")
+        q_quant(0, 0, 1, 2)
+        scores(1, 0)
+        scores(1, 1)
+        for part in range(4):
+            q_weave(0, 1, part, 4, "G")
+        for part in range(4):
+            v_weave(0, 1, part, 4, "G")
+
+        pre = {2: [lambda: v_quant(0, 0), lambda: v_quant(0, 1)]}
+        post = {
+            1: [
+                lambda: q_quant(0, 1, 0, 1),
+                lambda: transposes(1, 0, 0, "z", 2),
+                lambda: transposes(1, 0, 1, "z", 2),
+            ],
+            2: [
+                lambda: k_mul(1, 0, 0),
+                lambda: q_affine(1, 0, 0),
+            ],
+            3: [
+                lambda: k_mul(1, 0, 1),
+                lambda: q_affine(1, 0, 1),
+                lambda: k_quant(1, 0),
+                lambda: transposes(1, 1, 0, "z", 2),
+                lambda: [q_weave(1, 0, i, 4, "G") for i in range(4)],
+            ],
+            4: [
+                lambda: k_mul(1, 1, 0),
+                lambda: q_affine(1, 1, 0),
+                lambda: transposes(1, 1, 1, "z", 2),
+            ],
+            5: [
+                lambda: k_mul(1, 1, 1),
+                lambda: q_affine(1, 1, 1),
+                lambda: q_quant(1, 0, 0, 1),
+                lambda: k_quant(1, 1),
+                lambda: [v_weave(1, 0, i, 4, "G") for i in range(4)],
+                lambda: [v_weave(1, 1, i, 4, "G") for i in range(4)],
+                lambda: [q_weave(1, 1, i, 4, "G") for i in range(4)],
+            ],
+            6: [lambda: o_weave(0, 0, 4, "S")],
+            7: [lambda: o_weave(0, 1, 4, "S"), lambda: v_quant(1, 0)],
+            8: [
+                lambda: o_weave(0, 2, 4, "S"),
+                lambda: o_weave(0, 3, 4, "S"),
+                lambda: v_quant(1, 1), lambda: q_quant(1, 1, 0, 1)],
+            9: [lambda: o_quant(0, 0, 1), lambda: o_weave(1, 0, 4, "S")],
+            10: [lambda: o_weave(1, 1, 4, "S")],
+            11: [lambda: o_weave(1, 2, 4, "S")],
+            12: [lambda: o_weave(1, 3, 4, "S")],
+            13: [lambda: o_quant(1, 0, 1)],
+            14: [lambda: o_weave(2, 0, 2, "V"), lambda: o_weave(2, 1, 2, "V")],
+            15: [lambda: o_quant(2, 0, 1)],
+        }
+        for c in range(NCH + 1):
+            for f in pre.get(c, []):
+                f()
+            if c < NCH:
+                weights(c, 0)
+            if c + 2 < NCH:
+                scores(c + 2, 0)
+            if c + 1 < NCH:
+                gain(c + 1, 0)
+            if c >= 1:
+                p_quant(c - 1)
+            if c == 2:
+                attend(0)
+            if c >= 2:
+                attend(c - 1)
+            if c < NCH:
+                weights(c, 1)
+            if c + 2 < NCH:
+                scores(c + 2, 1)
+            if c + 1 < NCH:
+                gain(c + 1, 1)
+            if c < NCH:
+                silu(c)
+            if c >= 2:
+                gate(c - 2, 0, E)
+            for f in post.get(c, []):
+                f()
+        last = NCH - 1
+        gate(last, E // 2, E)
+        o_weave(3, 1, 2, "S")
+        gate(last, 0, E // 2)
+        o_weave(3, 0, 2, "V")
+        o_quant(3, 0, 2)
+        o_quant(3, 1, 2)

@@ -84,6 +84,8 @@ def tile_mossformersquaredrelugatedattention_x1_kernel(
         nc.scalar.activation(out=warm_o[:], in_=warm[:], func=ACT.Silu)
         ident = kt([P, P], F32, "ident")
         make_identity(nc, ident[:])
+        ident_b = kt([P, P], BF16, "ident_b")
+        nc.vector.tensor_copy(out=ident_b[:], in_=ident[:])
         g1_f = kt([P, 4], F32, "g1_f")
         b1_f = kt([P, 4], F32, "b1_f")
         r_f = kt([P, G * 4], F32, "r_f")
@@ -183,12 +185,28 @@ def tile_mossformersquaredrelugatedattention_x1_kernel(
             vc[b] = kt([P, G, E], U32, "vc%d" % b)
             vs[b] = kt([P, G, E], U8, "vs%d" % b)
 
-        def v_weave(b, g, part, nparts, eng):
-            if part == 0:
+        vw = {}
+
+        def v_weave(b, g, h):
+            bank = psum.tile([P, 256, 4], BF16, name="z", tag="z", bufs=2)
+            vw[b, g, h] = bank
+            for i in range(2):
+                e0 = 256 * h + 128 * i
+                nc.tensor.matmul(
+                    bank[:, 128 * i : 128 * (i + 1), :].rearrange("p n t -> p (n t)"),
+                    lhsT=ident_b[:],
+                    rhs=v_t[b, g][:, :, e0 : e0 + 128].rearrange("p t n -> p n t"),
+                    start=True,
+                    stop=True,
+                )
+
+        def v_copy(b, g, h):
+            if h == 0:
                 vb[b, g] = wt([P, E, 4], BF16, "vb", 2)
-            n = E // nparts
-            c = slice(n * part, n * (part + 1))
-            weave(eng, vb[b, g][:, c, :], v_t[b, g][:, :, c])
+            nc.scalar.copy(
+                out=vb[b, g][:, 256 * h : 256 * (h + 1), :].rearrange("p n t -> p (n t)"),
+                in_=vw[b, g, h][:].rearrange("p n t -> p (n t)"),
+            )
 
         def v_quant(b, g):
             nc.vector.quantize_mx(
@@ -319,93 +337,110 @@ def tile_mossformersquaredrelugatedattention_x1_kernel(
         transposes(0, 0, 1, "z", 2)
         transposes(0, 1, 0, "s", 4)
         transposes(0, 1, 1, "s", 4)
-        for part in range(4):
-            v_weave(0, 0, part, 4, "G")
         k_mul(0, 0, 0)
         q_affine(0, 0, 0)
         k_mul(0, 0, 1)
         q_affine(0, 0, 1)
-        q_weave(0, 0, 0, 2, "V")
-        q_quant(0, 0, 0, 2)
-        k_quant(0, 0)
         k_mul(0, 1, 0)
+        q_weave(0, 0, 0, 2, "V")
+        k_quant(0, 0)
+        q_quant(0, 0, 0, 2)
         k_mul(0, 1, 1)
-        scores(0, 0)
         q_affine(0, 1, 0)
+        v_weave(0, 0, 0)
+        scores(0, 0)
         gain(0, 0)
         k_quant(0, 1)
-        scores(0, 1)
-        q_affine(0, 1, 1)
-        gain(0, 1)
         q_weave(0, 0, 1, 2, "V")
+        scores(0, 1)
+        gain(0, 1)
+        q_affine(0, 1, 1)
         q_quant(0, 0, 1, 2)
+        v_copy(0, 0, 0)
+        v_weave(0, 0, 1)
         scores(1, 0)
         scores(1, 1)
-        for part in range(4):
-            q_weave(0, 1, part, 4, "G")
-        for part in range(4):
-            v_weave(0, 1, part, 4, "G")
 
-        pre = {2: [lambda: v_quant(0, 0), lambda: v_quant(0, 1)]}
         post = {
+            0: [
+                lambda: v_copy(0, 0, 1),
+                lambda: v_weave(0, 1, 0),
+                lambda: q_weave(0, 1, 0, 1, "V"),
+                lambda: v_copy(0, 1, 0),
+                lambda: v_weave(0, 1, 1),
+            ],
             1: [
+                lambda: v_copy(0, 1, 1),
                 lambda: q_quant(0, 1, 0, 1),
+                lambda: v_quant(0, 0),
                 lambda: transposes(1, 0, 0, "z", 2),
                 lambda: transposes(1, 0, 1, "z", 2),
             ],
             2: [
+                lambda: v_quant(0, 1),
+                lambda: attend(0),
+                lambda: attend(1),
                 lambda: k_mul(1, 0, 0),
+                lambda: k_mul(1, 0, 1),
                 lambda: q_affine(1, 0, 0),
             ],
             3: [
-                lambda: k_mul(1, 0, 1),
                 lambda: q_affine(1, 0, 1),
                 lambda: k_quant(1, 0),
                 lambda: transposes(1, 1, 0, "z", 2),
-                lambda: [q_weave(1, 0, i, 4, "G") for i in range(4)],
+                lambda: transposes(1, 1, 1, "z", 2),
+                lambda: q_weave(1, 0, 0, 2, "S"),
             ],
             4: [
                 lambda: k_mul(1, 1, 0),
                 lambda: q_affine(1, 1, 0),
-                lambda: transposes(1, 1, 1, "z", 2),
+                lambda: q_weave(1, 0, 1, 2, "V"),
+                lambda: k_mul(1, 1, 1),
             ],
             5: [
-                lambda: k_mul(1, 1, 1),
                 lambda: q_affine(1, 1, 1),
                 lambda: q_quant(1, 0, 0, 1),
                 lambda: k_quant(1, 1),
-                lambda: [v_weave(1, 0, i, 4, "G") for i in range(4)],
-                lambda: [v_weave(1, 1, i, 4, "G") for i in range(4)],
-                lambda: [q_weave(1, 1, i, 4, "G") for i in range(4)],
+                lambda: v_weave(1, 0, 0),
+                lambda: v_weave(1, 0, 1),
             ],
-            6: [lambda: o_weave(0, 0, 4, "S")],
-            7: [lambda: o_weave(0, 1, 4, "S"), lambda: v_quant(1, 0)],
+            6: [
+                lambda: v_copy(1, 0, 0),
+                lambda: v_copy(1, 0, 1),
+                lambda: v_weave(1, 1, 0),
+                lambda: v_weave(1, 1, 1),
+            ],
+            7: [
+                lambda: v_copy(1, 1, 0),
+                lambda: v_copy(1, 1, 1),
+                lambda: q_weave(1, 1, 0, 1, "V"),
+            ],
             8: [
-                lambda: o_weave(0, 2, 4, "S"),
-                lambda: o_weave(0, 3, 4, "S"),
-                lambda: v_quant(1, 1), lambda: q_quant(1, 1, 0, 1)],
-            9: [lambda: o_quant(0, 0, 1), lambda: o_weave(1, 0, 4, "S")],
-            10: [lambda: o_weave(1, 1, 4, "S")],
-            11: [lambda: o_weave(1, 2, 4, "S")],
-            12: [lambda: o_weave(1, 3, 4, "S")],
-            13: [lambda: o_quant(1, 0, 1)],
-            14: [lambda: o_weave(2, 0, 2, "V"), lambda: o_weave(2, 1, 2, "V")],
-            15: [lambda: o_quant(2, 0, 1)],
+                lambda: v_quant(1, 0),
+                lambda: v_quant(1, 1),
+                lambda: o_weave(0, 0, 4, "S"),
+                lambda: o_weave(0, 1, 4, "S"),
+            ],
+            9: [lambda: o_weave(0, 2, 4, "S"), lambda: q_quant(1, 1, 0, 1)],
+            10: [lambda: o_weave(0, 3, 4, "S")],
+            11: [lambda: o_weave(1, 0, 4, "S"), lambda: o_weave(1, 1, 2, "V")],
+            12: [lambda: o_quant(0, 0, 1), lambda: o_weave(1, 1, 4, "S")],
+            13: [],
+            14: [lambda: o_weave(2, 0, 2, "V"), lambda: o_weave(2, 2, 4, "S"), lambda: o_weave(2, 3, 4, "S")],
+            15: [lambda: o_quant(1, 0, 1), lambda: o_quant(2, 0, 1)],
         }
         for c in range(NCH + 1):
-            for f in pre.get(c, []):
-                f()
+            if c >= 1:
+                p_quant(c - 1)
+            if c == 3:
+                gate(0, 0, E)
             if c < NCH:
                 weights(c, 0)
             if c + 2 < NCH:
                 scores(c + 2, 0)
             if c + 1 < NCH:
                 gain(c + 1, 0)
-            if c >= 1:
-                p_quant(c - 1)
-            if c == 2:
-                attend(0)
-            if c >= 2:
+            if c >= 3:
                 attend(c - 1)
             if c < NCH:
                 weights(c, 1)
@@ -415,7 +450,7 @@ def tile_mossformersquaredrelugatedattention_x1_kernel(
                 gain(c + 1, 1)
             if c < NCH:
                 silu(c)
-            if c >= 2:
+            if c >= 3:
                 gate(c - 2, 0, E)
             for f in post.get(c, []):
                 f()

@@ -73,8 +73,8 @@ def tile_mossformersquaredrelugatedattention_x1_kernel(
 
         load_z(0)
         load_v(0)
-        load_z(1)
         load_u(0)
+        load_z(1)
         load_v(1)
         load_u(1)
 
@@ -161,7 +161,8 @@ def tile_mossformersquaredrelugatedattention_x1_kernel(
             weave(eng, qb[b, g][:, c, :], qp[b, g][:, :, c])
 
         def weave(eng, dst, src):
-            src = src.rearrange("p t n -> p n t")
+            dst = dst.rearrange("p (c i) t -> p c t i", i=4)
+            src = src.rearrange("p t (c i) -> p c t i", i=4)
             if eng == "V":
                 nc.vector.tensor_copy(out=dst, in_=src)
             elif eng == "S":
@@ -289,7 +290,9 @@ def tile_mossformersquaredrelugatedattention_x1_kernel(
             sl[c] = wt([P, E], F32, "sl", 4)
             nc.scalar.activation(out=sl[c][:], in_=u_t[b, ig][:, t, :], func=ACT.Silu)
 
-        def gate(c, e0, e1):
+        split = (3, 7, 11)
+
+        def gate(c, e0, e1, store=True):
             b, ig, t = coords(c)
             k = c // 4
             if t == 0:
@@ -302,7 +305,14 @@ def tile_mossformersquaredrelugatedattention_x1_kernel(
                 op0=ALU.mult,
                 op1=ALU.mult,
             )
-            nc.sync.dma_start(out=rows(out_0, b, ig)[:, t, e0:e1], in_=R[k][:, t, e0:e1])
+            if store:
+                store_out(c, e0, e1)
+
+        def store_out(c, e0, e1):
+            b, ig, t = coords(c)
+            nc.sync.dma_start(
+                out=rows(out_0, b, ig)[:, t, e0:e1], in_=R[c // 4][:, t, e0:e1]
+            )
 
         def o_weave(k, part, nparts, eng):
             if k not in obf:
@@ -347,95 +357,95 @@ def tile_mossformersquaredrelugatedattention_x1_kernel(
         q_quant(0, 0, 0, 2)
         k_mul(0, 1, 1)
         q_affine(0, 1, 0)
-        v_weave(0, 0, 0)
         scores(0, 0)
         gain(0, 0)
-        k_quant(0, 1)
         q_weave(0, 0, 1, 2, "V")
+        k_quant(0, 1)
         scores(0, 1)
         gain(0, 1)
         q_affine(0, 1, 1)
         q_quant(0, 0, 1, 2)
-        v_copy(0, 0, 0)
+        v_weave(0, 0, 0)
         v_weave(0, 0, 1)
+        v_copy(0, 0, 0)
         scores(1, 0)
         scores(1, 1)
 
+        pre = {
+            1: [lambda: p_quant(0), lambda: q_weave(0, 1, 0, 1, "V")],
+            2: [lambda: v_quant(0, 0), lambda: q_quant(0, 1, 0, 1), lambda: v_quant(0, 1), lambda: attend(0), lambda: attend(1)],
+            3: [lambda: gate(0, 0, E)],
+            4: [lambda: k_quant(1, 0)],
+            6: [lambda: k_quant(1, 1), lambda: q_quant(1, 0, 0, 1)],
+            8: [lambda: o_quant(0, 0, 1)],
+            9: [lambda: v_quant(1, 0), lambda: v_quant(1, 1)],
+            10: [lambda: q_quant(1, 1, 0, 2)],
+            12: [lambda: q_quant(1, 1, 1, 2), lambda: o_quant(1, 0, 1)],
+        }
         post = {
             0: [
                 lambda: v_copy(0, 0, 1),
                 lambda: v_weave(0, 1, 0),
-                lambda: q_weave(0, 1, 0, 1, "V"),
                 lambda: v_copy(0, 1, 0),
                 lambda: v_weave(0, 1, 1),
+                lambda: v_copy(0, 1, 1),
             ],
             1: [
-                lambda: v_copy(0, 1, 1),
-                lambda: q_quant(0, 1, 0, 1),
-                lambda: v_quant(0, 0),
                 lambda: transposes(1, 0, 0, "z", 2),
-                lambda: transposes(1, 0, 1, "z", 2),
             ],
             2: [
-                lambda: v_quant(0, 1),
-                lambda: attend(0),
-                lambda: attend(1),
+                lambda: transposes(1, 0, 1, "z", 2),
                 lambda: k_mul(1, 0, 0),
-                lambda: k_mul(1, 0, 1),
                 lambda: q_affine(1, 0, 0),
             ],
             3: [
+                lambda: k_mul(1, 0, 1),
                 lambda: q_affine(1, 0, 1),
-                lambda: k_quant(1, 0),
                 lambda: transposes(1, 1, 0, "z", 2),
                 lambda: transposes(1, 1, 1, "z", 2),
-                lambda: q_weave(1, 0, 0, 2, "S"),
             ],
             4: [
                 lambda: k_mul(1, 1, 0),
-                lambda: q_affine(1, 1, 0),
-                lambda: q_weave(1, 0, 1, 2, "V"),
                 lambda: k_mul(1, 1, 1),
+                lambda: q_weave(1, 0, 0, 2, "V"),
             ],
             5: [
-                lambda: q_affine(1, 1, 1),
-                lambda: q_quant(1, 0, 0, 1),
-                lambda: k_quant(1, 1),
+                lambda: q_weave(1, 0, 1, 2, "V"),
+                lambda: q_affine(1, 1, 0),
                 lambda: v_weave(1, 0, 0),
-                lambda: v_weave(1, 0, 1),
             ],
             6: [
+                lambda: q_affine(1, 1, 1),
                 lambda: v_copy(1, 0, 0),
-                lambda: v_copy(1, 0, 1),
+                lambda: v_weave(1, 0, 1),
                 lambda: v_weave(1, 1, 0),
-                lambda: v_weave(1, 1, 1),
             ],
             7: [
+                lambda: v_copy(1, 0, 1),
                 lambda: v_copy(1, 1, 0),
-                lambda: v_copy(1, 1, 1),
-                lambda: q_weave(1, 1, 0, 1, "V"),
+                lambda: v_weave(1, 1, 1),
             ],
             8: [
-                lambda: v_quant(1, 0),
-                lambda: v_quant(1, 1),
-                lambda: o_weave(0, 0, 4, "S"),
-                lambda: o_weave(0, 1, 4, "S"),
+                lambda: v_copy(1, 1, 1),
+                lambda: q_weave(1, 1, 0, 2, "S"),
             ],
-            9: [lambda: o_weave(0, 2, 4, "S"), lambda: q_quant(1, 1, 0, 1)],
-            10: [lambda: o_weave(0, 3, 4, "S")],
-            11: [lambda: o_weave(1, 0, 4, "S"), lambda: o_weave(1, 1, 2, "V")],
-            12: [lambda: o_quant(0, 0, 1), lambda: o_weave(1, 1, 4, "S")],
-            13: [],
-            14: [lambda: o_weave(2, 0, 2, "V"), lambda: o_weave(2, 2, 4, "S"), lambda: o_weave(2, 3, 4, "S")],
-            15: [lambda: o_quant(1, 0, 1), lambda: o_quant(2, 0, 1)],
+            9: [lambda: q_weave(1, 1, 1, 2, "S")],
         }
         for c in range(NCH + 1):
-            if c >= 1:
+            if c not in (5, 9, 13) and c >= 2:
                 p_quant(c - 1)
-            if c == 3:
-                gate(0, 0, E)
+            for f in pre.get(c, []):
+                f()
+            for k in range(3):
+                i = c - (4 * k + 5)
+                if 0 <= i < 2:
+                    gate(4 * k + 3, 256 * i, 256 * (i + 1))
+                    o_weave(k, 2 * i, 4, "G")
+                    o_weave(k, 2 * i + 1, 4, "G")
             if c < NCH:
                 weights(c, 0)
+            if c in (5, 9, 13):
+                p_quant(c - 1)
             if c + 2 < NCH:
                 scores(c + 2, 0)
             if c + 1 < NCH:
@@ -448,13 +458,14 @@ def tile_mossformersquaredrelugatedattention_x1_kernel(
                 scores(c + 2, 1)
             if c + 1 < NCH:
                 gain(c + 1, 1)
-            if c < NCH:
-                silu(c)
-            if c >= 3:
+            if 1 <= c:
+                silu(c - 1)
+            if c >= 3 and c - 2 not in split:
                 gate(c - 2, 0, E)
             for f in post.get(c, []):
                 f()
         last = NCH - 1
+        o_quant(2, 0, 1)
         gate(last, E // 2, E)
         o_weave(3, 1, 2, "S")
         gate(last, 0, E // 2)

@@ -57,9 +57,12 @@ def tile_mossformersquaredrelugatedattention_x1_kernel(
             for g in range(G):
                 for h in range(2):
                     z_t[b, g, h] = kt([P, 2, D], BF16, "z%d%d%d" % (b, g, h))
-                    nc.sync.dma_start(
-                        out=z_t[b, g, h][:], in_=rows(z, b, g)[:, 2 * h : 2 * h + 2, :]
-                    )
+                    parts = [0, 1, 2] if (b, g, h) == (0, 0, 0) else [0, 2]
+                    for i, j in zip(parts, parts[1:]):
+                        nc.sync.dma_start(
+                            out=z_t[b, g, h][:, i:j, :],
+                            in_=rows(z, b, g)[:, 2 * h + i : 2 * h + j, :],
+                        )
 
         def load_v(b):
             for g in range(G):
@@ -82,6 +85,8 @@ def tile_mossformersquaredrelugatedattention_x1_kernel(
         warm_o = kt([P, 1], F32, "warm_o")
         nc.vector.memset(warm[:], 0.0)
         nc.scalar.activation(out=warm_o[:], in_=warm[:], func=ACT.Silu)
+        zeros = kt([P, 512], BF16, "zeros")
+        nc.vector.memset(zeros[:], 0.0)
         ident = kt([P, P], F32, "ident")
         make_identity(nc, ident[:])
         ident_b = kt([P, P], BF16, "ident_b")
@@ -89,15 +94,12 @@ def tile_mossformersquaredrelugatedattention_x1_kernel(
         g1_f = kt([P, 4], F32, "g1_f")
         b1_f = kt([P, 4], F32, "b1_f")
         r_f = kt([P, G * 4], F32, "r_f")
-        nc.vector.tensor_copy(out=g1_f[:], in_=g1_b[:])
-        nc.vector.tensor_copy(out=b1_f[:], in_=b1_b[:])
-        nc.vector.tensor_scalar(
-            out=r_f[:],
-            in0=r_b[:].rearrange("p g t -> p (g t)"),
-            scalar1=1.0 / D,
-            scalar2=None,
-            op0=ALU.mult,
-        )
+        nc.scalar.copy(out=g1_f[:], in_=g1_b[:])
+        nc.scalar.copy(out=b1_f[:], in_=b1_b[:])
+
+        for i in range(5):
+            bank = ps("o", 2)
+            nc.tensor.matmul(bank[:], lhsT=zeros[:, 0:P], rhs=zeros[:], start=True, stop=True)
 
         kc, ks, qc, qs = {}, {}, {}, {}
         for b in range(B):
@@ -287,12 +289,12 @@ def tile_mossformersquaredrelugatedattention_x1_kernel(
 
         def silu(c):
             b, ig, t = coords(c)
-            sl[c] = wt([P, E], F32, "sl", 4)
-            nc.scalar.activation(out=sl[c][:], in_=u_t[b, ig][:, t, :], func=ACT.Silu)
+            pair = wt([P, 2, E], F32, "sl", 3)
+            nc.scalar.activation(out=pair[:], in_=u_t[b, ig][:, t : t + 2, :], func=ACT.Silu)
+            sl[c] = pair[:, 0, :]
+            sl[c + 1] = pair[:, 1, :]
 
-        split = (3, 7, 11)
-
-        def gate(c, e0, e1, store=True):
+        def gate(c, e0, e1):
             b, ig, t = coords(c)
             k = c // 4
             if t == 0:
@@ -305,14 +307,7 @@ def tile_mossformersquaredrelugatedattention_x1_kernel(
                 op0=ALU.mult,
                 op1=ALU.mult,
             )
-            if store:
-                store_out(c, e0, e1)
-
-        def store_out(c, e0, e1):
-            b, ig, t = coords(c)
-            nc.sync.dma_start(
-                out=rows(out_0, b, ig)[:, t, e0:e1], in_=R[c // 4][:, t, e0:e1]
-            )
+            nc.sync.dma_start(out=rows(out_0, b, ig)[:, t, e0:e1], in_=R[k][:, t, e0:e1])
 
         def o_weave(k, part, nparts, eng):
             if k not in obf:
@@ -351,6 +346,7 @@ def tile_mossformersquaredrelugatedattention_x1_kernel(
         q_affine(0, 0, 0)
         k_mul(0, 0, 1)
         q_affine(0, 0, 1)
+        nc.scalar.mul(out=r_f[:], in_=r_b[:].rearrange("p g t -> p (g t)"), mul=1.0 / D)
         k_mul(0, 1, 0)
         q_weave(0, 0, 0, 2, "V")
         k_quant(0, 0)
@@ -359,31 +355,38 @@ def tile_mossformersquaredrelugatedattention_x1_kernel(
         q_affine(0, 1, 0)
         scores(0, 0)
         gain(0, 0)
-        q_weave(0, 0, 1, 2, "V")
         k_quant(0, 1)
         scores(0, 1)
         gain(0, 1)
+        q_weave(0, 0, 1, 2, "V")
         q_affine(0, 1, 1)
-        q_quant(0, 0, 1, 2)
-        v_weave(0, 0, 0)
-        v_weave(0, 0, 1)
-        v_copy(0, 0, 0)
         scores(1, 0)
         scores(1, 1)
+        v_weave(0, 0, 0)
+        v_weave(0, 0, 1)
 
         pre = {
-            1: [lambda: p_quant(0), lambda: q_weave(0, 1, 0, 1, "V")],
-            2: [lambda: v_quant(0, 0), lambda: q_quant(0, 1, 0, 1), lambda: v_quant(0, 1), lambda: attend(0), lambda: attend(1)],
+            0: [lambda: q_quant(0, 0, 1, 2)],
+            1: [lambda: q_weave(0, 1, 0, 2, "V"), lambda: p_quant(0), lambda: q_weave(0, 1, 1, 2, "V")],
+            2: [
+                lambda: v_quant(0, 0),
+                lambda: p_quant(1),
+                lambda: q_quant(0, 1, 0, 1),
+                lambda: v_quant(0, 1),
+                lambda: attend(0),
+                lambda: attend(1),
+            ],
             3: [lambda: gate(0, 0, E)],
             4: [lambda: k_quant(1, 0)],
             6: [lambda: k_quant(1, 1), lambda: q_quant(1, 0, 0, 1)],
-            8: [lambda: o_quant(0, 0, 1)],
             9: [lambda: v_quant(1, 0), lambda: v_quant(1, 1)],
             10: [lambda: q_quant(1, 1, 0, 2)],
-            12: [lambda: q_quant(1, 1, 1, 2), lambda: o_quant(1, 0, 1)],
+            12: [lambda: q_quant(1, 1, 1, 2), lambda: o_quant(0, 0, 1)],
+            15: [lambda: o_quant(1, 0, 1)],
         }
         post = {
             0: [
+                lambda: v_copy(0, 0, 0),
                 lambda: v_copy(0, 0, 1),
                 lambda: v_weave(0, 1, 0),
                 lambda: v_copy(0, 1, 0),
@@ -402,15 +405,15 @@ def tile_mossformersquaredrelugatedattention_x1_kernel(
                 lambda: k_mul(1, 0, 1),
                 lambda: q_affine(1, 0, 1),
                 lambda: transposes(1, 1, 0, "z", 2),
-                lambda: transposes(1, 1, 1, "z", 2),
             ],
             4: [
+                lambda: transposes(1, 1, 1, "z", 2),
                 lambda: k_mul(1, 1, 0),
-                lambda: k_mul(1, 1, 1),
                 lambda: q_weave(1, 0, 0, 2, "V"),
             ],
             5: [
                 lambda: q_weave(1, 0, 1, 2, "V"),
+                lambda: k_mul(1, 1, 1),
                 lambda: q_affine(1, 1, 0),
                 lambda: v_weave(1, 0, 0),
             ],
@@ -424,28 +427,28 @@ def tile_mossformersquaredrelugatedattention_x1_kernel(
                 lambda: v_copy(1, 0, 1),
                 lambda: v_copy(1, 1, 0),
                 lambda: v_weave(1, 1, 1),
+                lambda: q_weave(1, 1, 0, 2, "V"),
             ],
             8: [
                 lambda: v_copy(1, 1, 1),
-                lambda: q_weave(1, 1, 0, 2, "S"),
+                lambda: o_weave(0, 0, 4, "S"),
+                lambda: q_weave(1, 1, 1, 2, "V"),
             ],
-            9: [lambda: q_weave(1, 1, 1, 2, "S")],
+            9: [lambda: o_weave(0, 1, 4, "S"), lambda: o_weave(0, 2, 4, "S")],
+            10: [lambda: o_weave(0, 3, 4, "S")],
+            11: [lambda: o_weave(1, 0, 4, "S")],
+            12: [lambda: o_weave(1, 1, 4, "S")],
+            13: [lambda: o_weave(1, 2, 4, "S"), lambda: o_weave(1, 3, 4, "S")],
+            14: [lambda: o_weave(2, 0, 2, "V"), lambda: o_weave(2, 2, 4, "S")],
+            15: [lambda: o_weave(2, 3, 4, "S")],
         }
         for c in range(NCH + 1):
-            if c not in (5, 9, 13) and c >= 2:
+            if c >= 3:
                 p_quant(c - 1)
             for f in pre.get(c, []):
                 f()
-            for k in range(3):
-                i = c - (4 * k + 5)
-                if 0 <= i < 2:
-                    gate(4 * k + 3, 256 * i, 256 * (i + 1))
-                    o_weave(k, 2 * i, 4, "G")
-                    o_weave(k, 2 * i + 1, 4, "G")
             if c < NCH:
                 weights(c, 0)
-            if c in (5, 9, 13):
-                p_quant(c - 1)
             if c + 2 < NCH:
                 scores(c + 2, 0)
             if c + 1 < NCH:
@@ -458,9 +461,9 @@ def tile_mossformersquaredrelugatedattention_x1_kernel(
                 scores(c + 2, 1)
             if c + 1 < NCH:
                 gain(c + 1, 1)
-            if 1 <= c:
+            if c % 2 == 1:
                 silu(c - 1)
-            if c >= 3 and c - 2 not in split:
+            if c >= 3:
                 gate(c - 2, 0, E)
             for f in post.get(c, []):
                 f()

@@ -85,8 +85,6 @@ def tile_mossformersquaredrelugatedattention_x1_kernel(
         warm_o = kt([P, 1], F32, "warm_o")
         nc.vector.memset(warm[:], 0.0)
         nc.scalar.activation(out=warm_o[:], in_=warm[:], func=ACT.Silu)
-        zeros = kt([P, 512], BF16, "zeros")
-        nc.vector.memset(zeros[:], 0.0)
         ident = kt([P, P], F32, "ident")
         make_identity(nc, ident[:])
         ident_b = kt([P, P], BF16, "ident_b")
@@ -96,10 +94,6 @@ def tile_mossformersquaredrelugatedattention_x1_kernel(
         r_f = kt([P, G * 4], F32, "r_f")
         nc.scalar.copy(out=g1_f[:], in_=g1_b[:])
         nc.scalar.copy(out=b1_f[:], in_=b1_b[:])
-
-        for i in range(5):
-            bank = ps("o", 2)
-            nc.tensor.matmul(bank[:], lhsT=zeros[:, 0:P], rhs=zeros[:], start=True, stop=True)
 
         kc, ks, qc, qs = {}, {}, {}, {}
         for b in range(B):
@@ -218,7 +212,7 @@ def tile_mossformersquaredrelugatedattention_x1_kernel(
                 in_=vb[b, g][:].rearrange("p n t -> p (n t)"),
             )
 
-        sb, wv, pb, pc, psc, ob, sl, R, obf = {}, {}, {}, {}, {}, {}, {}, {}, {}
+        sb, wv, pb, pc, psc, ob, sl, R, obf, oc, osc = {}, {}, {}, {}, {}, {}, {}, {}, {}, {}, {}
 
         def coords(c):
             return c // (4 * G), (c // 4) % G, c % 4
@@ -320,22 +314,27 @@ def tile_mossformersquaredrelugatedattention_x1_kernel(
             b, ig = k // G, k % G
             n = E // nparts
             e0 = n * part
-            oc = wt([P, n], U32, "oc%d" % nparts, 2)
-            osc = wt([P, n], U8, "osc%d" % nparts, 2)
+            if k not in oc:
+                oc[k] = wt([P, E], U32, "oc", 2)
+                osc[k] = wt([P, E], U8, "osc", 2)
+            c = slice(e0, e0 + n)
             nc.vector.quantize_mx(
-                out=oc[:].bitcast(FP8X4),
-                scales=osc[:],
-                in_=obf[k][:, e0 : e0 + n, :].rearrange("p n t -> p (n t)"),
+                out=oc[k][:, c].bitcast(FP8X4),
+                scales=osc[k][:, c],
+                in_=obf[k][:, c, :].rearrange("p n t -> p (n t)"),
             )
             m = slice(E * b + e0, E * b + e0 + n)
             nc.sync.dma_start(
                 out=out_1[ig, :, m, :].rearrange("p m t -> p (m t)").bitcast(I32),
-                in_=oc[:].bitcast(I32),
+                in_=oc[k][:, c].bitcast(I32),
             )
+
+        def store_scales(k):
+            b, ig = k // G, k % G
             for quad in range(4):
                 nc.sync.dma_start(
-                    out=out_2[ig, 4 * quad : 4 * quad + 4, m].bitcast(I32),
-                    in_=osc[32 * quad : 32 * quad + 4, :].bitcast(I32),
+                    out=out_2[ig, 4 * quad : 4 * quad + 4, E * b : E * (b + 1)].bitcast(I32),
+                    in_=osc[k][32 * quad : 32 * quad + 4, :].bitcast(I32),
                 )
 
         transposes(0, 0, 0, "z", 2)
@@ -381,8 +380,8 @@ def tile_mossformersquaredrelugatedattention_x1_kernel(
             6: [lambda: k_quant(1, 1), lambda: q_quant(1, 0, 0, 1)],
             9: [lambda: v_quant(1, 0), lambda: v_quant(1, 1)],
             10: [lambda: q_quant(1, 1, 0, 2)],
-            12: [lambda: q_quant(1, 1, 1, 2), lambda: o_quant(0, 0, 1)],
-            15: [lambda: o_quant(1, 0, 1)],
+            12: [lambda: q_quant(1, 1, 1, 2), lambda: o_quant(0, 0, 1), lambda: store_scales(0)],
+            15: [lambda: o_quant(1, 0, 1), lambda: store_scales(1)],
         }
         post = {
             0: [
@@ -468,10 +467,12 @@ def tile_mossformersquaredrelugatedattention_x1_kernel(
             for f in post.get(c, []):
                 f()
         last = NCH - 1
-        o_quant(2, 0, 1)
         gate(last, E // 2, E)
         o_weave(3, 1, 2, "S")
         gate(last, 0, E // 2)
+        o_quant(2, 0, 1)
+        store_scales(2)
         o_weave(3, 0, 2, "V")
-        o_quant(3, 0, 2)
         o_quant(3, 1, 2)
+        o_quant(3, 0, 2)
+        store_scales(3)

from contextlib import ExitStack

import concourse.mybir as mybir
from concourse.masks import make_identity

B, T, D, E = 2, 1024, 512, 512
FLOPS = 2 * B * T * T * (D + E)

F32 = mybir.dt.float32
BF16 = mybir.dt.bfloat16
I32 = mybir.dt.int32
U32 = mybir.dt.uint32
U8 = mybir.dt.uint8
FP8X4 = mybir.dt.float8_e4m3fn_x4
ACT = mybir.ActivationFunctionType
ALU = mybir.AluOpType

P = 128
G = T // 512
NCH = B * G * 4


def tile_mossformersquaredrelugatedattention_x1_kernel(
    tc, z, g1, b1, g2, r, v, u, out_0, out_1, out_2
):
    nc = tc.nc
    with ExitStack() as ctx:
        keep = ctx.enter_context(tc.tile_pool(name="keep", bufs=1))
        work = ctx.enter_context(tc.tile_pool(name="work", bufs=2))
        psum = ctx.enter_context(tc.psum_pool(name="psum", bufs=2))
        ctx.enter_context(tc.manual_schedule())

        def kt(shape, dt, name):
            return keep.tile(shape, dt, name=name, align_bytes=64)

        def wt(shape, dt, name, bufs):
            return work.tile(shape, dt, name=name, tag=name, bufs=bufs, align_bytes=64)

        def ps(name, bufs):
            return psum.tile([P, 512], F32, name=name, tag=name, bufs=bufs)

        g2_t = kt([P, 2, 2], BF16, "g2_t")
        g1_b = kt([P, 4], BF16, "g1_b")
        b1_b = kt([P, 4], BF16, "b1_b")
        r_b = kt([P, G, 4], BF16, "r_b")
        nc.scalar.dma_start(out=g2_t[:], in_=g2.rearrange("(p u e) -> p u e", u=2, e=2))
        nc.scalar.dma_start(out=g1_b[:], in_=g1.rearrange("(p t) -> p t", t=4))
        nc.scalar.dma_start(out=b1_b[:], in_=b1.rearrange("(p t) -> p t", t=4))
        nc.scalar.dma_start(out=r_b[:], in_=r.rearrange("(g p t) -> p g t", g=G, t=4))

        def rows(x, b, g):
            return x[b, 512 * g : 512 * (g + 1), :].rearrange("(p t) d -> p t d", t=4)

        z_t, v_t, u_t = {}, {}, {}

        def load_z(b):
            for g in range(G):
                for h in range(2):
                    z_t[b, g, h] = kt([P, 2, D], BF16, "z%d%d%d" % (b, g, h))
                    parts = [0, 1, 2] if (b, g, h) == (0, 0, 0) else [0, 2]
                    for i, j in zip(parts, parts[1:]):
                        nc.sync.dma_start(
                            out=z_t[b, g, h][:, i:j, :],
                            in_=rows(z, b, g)[:, 2 * h + i : 2 * h + j, :],
                        )

        def load_v(b):
            for g in range(G):
                v_t[b, g] = kt([P, 4, E], BF16, "v%d%d" % (b, g))
                nc.sync.dma_start(out=v_t[b, g][:], in_=rows(v, b, g))

        def load_u(b):
            for g in range(G):
                u_t[b, g] = kt([P, 4, E], BF16, "u%d%d" % (b, g))
                nc.sync.dma_start(out=u_t[b, g][:], in_=rows(u, b, g))

        load_z(0)
        load_v(0)
        load_u(0)
        load_z(1)
        load_v(1)
        load_u(1)

        warm = kt([P, 1], F32, "warm")
        warm_o = kt([P, 1], F32, "warm_o")
        nc.vector.memset(warm[:], 0.0)
        nc.scalar.activation(out=warm_o[:], in_=warm[:], func=ACT.Silu)
        ident = kt([P, P], F32, "ident")
        make_identity(nc, ident[:])
        ident_b = kt([P, P], BF16, "ident_b")
        nc.vector.tensor_copy(out=ident_b[:], in_=ident[:])
        g1_f = kt([P, 4], F32, "g1_f")
        b1_f = kt([P, 4], F32, "b1_f")
        r_f = kt([P, G * 4], F32, "r_f")
        nc.scalar.copy(out=g1_f[:], in_=g1_b[:])
        nc.scalar.copy(out=b1_f[:], in_=b1_b[:])

        kc, ks, qc, qs = {}, {}, {}, {}
        for b in range(B):
            kc[b] = kt([P, T], U32, "kc%d" % b)
            ks[b] = kt([P, T], U8, "ks%d" % b)
            qc[b] = kt([P, T], U32, "qc%d" % b)
            qs[b] = kt([P, T], U8, "qs%d" % b)
        zt, kb, qp, qb = {}, {}, {}, {}

        def transposes(b, g, h, tag, bufs):
            bank = ps(tag, bufs)
            zt[b, g, h] = bank
            words = z_t[b, g, h][:].rearrange("p t d -> p (t d)").bitcast(F32)
            for s in range(2):
                for w in range(2):
                    nc.tensor.transpose(
                        bank[:, 256 * w + 128 * s : 256 * w + 128 * (s + 1)],
                        words[:, 256 * s + w : 256 * (s + 1) : 2],
                        ident[:],
                    )

        def k_mul(b, g, h):
            if h == 0:
                kb[b, g] = wt([P, 512, 4], BF16, "kb", 2)
            src = zt[b, g, h][:].bitcast(BF16).rearrange("p (u n e) -> p n u e", u=2, e=2)
            nc.vector.tensor_tensor(
                out=kb[b, g][:, 256 * h : 256 * (h + 1), :].rearrange(
                    "p n (u e) -> p n u e", u=2
                ),
                in0=src,
                in1=g2_t[:].unsqueeze(1).to_broadcast([P, 256, 2, 2]),
                op=ALU.mult,
            )

        def k_quant(b, g):
            c = slice(512 * g, 512 * (g + 1))
            nc.vector.quantize_mx(
                out=kc[b][:, c].bitcast(FP8X4),
                scales=ks[b][:, c],
                in_=kb[b, g][:].rearrange("p n t -> p (n t)"),
            )

        def q_affine(b, g, h):
            if h == 0:
                qp[b, g] = wt([P, 4, 512], BF16, "qp", 2)
            src = zt[b, g, h][:].bitcast(BF16).rearrange("p (u n e) -> p u n e", u=2, e=2)
            for t in range(4):
                nc.scalar.activation(
                    out=qp[b, g][:, t, 256 * h : 256 * (h + 1)],
                    in_=src[:, t // 2, :, t % 2],
                    func=ACT.Identity,
                    scale=g1_f[:, t : t + 1],
                    bias=b1_f[:, t : t + 1],
                )

        def q_weave(b, g, part, nparts, eng):
            if part == 0:
                qb[b, g] = wt([P, 512, 4], BF16, "qb", 2)
            n = 512 // nparts
            c = slice(n * part, n * (part + 1))
            weave(eng, qb[b, g][:, c, :], qp[b, g][:, :, c])

        def weave(eng, dst, src):
            dst = dst.rearrange("p (c i) t -> p c t i", i=4)
            src = src.rearrange("p t (c i) -> p c t i", i=4)
            if eng == "V":
                nc.vector.tensor_copy(out=dst, in_=src)
            elif eng == "S":
                nc.scalar.copy(out=dst, in_=src)
            else:
                nc.gpsimd.tensor_scalar(
                    out=dst, in0=src, scalar1=1.0, scalar2=1.0, op0=ALU.mult, op1=ALU.mult
                )

        def q_quant(b, g, part, nparts):
            n = 512 // nparts
            c = slice(512 * g + n * part, 512 * g + n * (part + 1))
            nc.vector.quantize_mx(
                out=qc[b][:, c].bitcast(FP8X4),
                scales=qs[b][:, c],
                in_=qb[b, g][:, n * part : n * (part + 1), :].rearrange("p n t -> p (n t)"),
            )

        vc, vs, vb = {}, {}, {}
        for b in range(B):
            vc[b] = kt([P, G, E], U32, "vc%d" % b)
            vs[b] = kt([P, G, E], U8, "vs%d" % b)

        vw = {}

        def v_weave(b, g, h):
            bank = psum.tile([P, 256, 4], BF16, name="z", tag="z", bufs=2)
            vw[b, g, h] = bank
            for i in range(2):
                e0 = 256 * h + 128 * i
                nc.tensor.matmul(
                    bank[:, 128 * i : 128 * (i + 1), :].rearrange("p n t -> p (n t)"),
                    lhsT=ident_b[:],
                    rhs=v_t[b, g][:, :, e0 : e0 + 128].rearrange("p t n -> p n t"),
                    start=True,
                    stop=True,
                )

        def v_copy(b, g, h):
            if h == 0:
                vb[b, g] = wt([P, E, 4], BF16, "vb", 2)
            nc.scalar.copy(
                out=vb[b, g][:, 256 * h : 256 * (h + 1), :].rearrange("p n t -> p (n t)"),
                in_=vw[b, g, h][:].rearrange("p n t -> p (n t)"),
            )

        def v_quant(b, g):
            nc.vector.quantize_mx(
                out=vc[b][:, g, :].bitcast(FP8X4),
                scales=vs[b][:, g, :],
                in_=vb[b, g][:].rearrange("p n t -> p (n t)"),
            )

        sb, wv, pb, pc, psc, ob, sl, R, obf, oc, osc = {}, {}, {}, {}, {}, {}, {}, {}, {}, {}, {}

        def coords(c):
            return c // (4 * G), (c // 4) % G, c % 4

        def scores(c, jg):
            b = coords(c)[0]
            q0 = 128 * (c % (4 * G))
            bank = ps("s", 4)
            sb[c, jg] = bank
            for t in range(4):
                k0 = 512 * jg + 128 * t
                nc.tensor.matmul_mx(
                    out=bank[:, 128 * t : 128 * (t + 1)],
                    lhsT=kc[b][:, k0 : k0 + 128].bitcast(FP8X4),
                    lhsT_scale=ks[b][:, k0 : k0 + 128],
                    rhs=qc[b][:, q0 : q0 + 128].bitcast(FP8X4),
                    rhs_scale=qs[b][:, q0 : q0 + 128],
                    start=True,
                    stop=True,
                )

        def gain(c, jg):
            wv[c, jg] = wt([P, 512], F32, "wv", 4)
            for t in range(4):
                n = slice(128 * t, 128 * (t + 1))
                nc.scalar.activation(
                    out=wv[c, jg][:, n],
                    in_=sb[c, jg][:, n],
                    func=ACT.Copy,
                    scale=r_f[:, 4 * jg + t : 4 * jg + t + 1],
                )

        def weights(c, jg):
            if jg == 0:
                pb[c] = wt([P, G, 128, 4], BF16, "pb", 3)
            nc.vector.scalar_tensor_tensor(
                out=pb[c][:, jg, :, :],
                in0=sb[c, jg][:].rearrange("p (t n) -> p n t", t=4),
                scalar=0.0,
                in1=wv[c, jg][:].rearrange("p (t n) -> p n t", t=4),
                op0=ALU.max,
                op1=ALU.mult,
            )

        def p_quant(c):
            pc[c] = wt([P, G * 128], U32, "pc", 4)
            psc[c] = wt([P, G * 128], U8, "psc", 4)
            nc.vector.quantize_mx(
                out=pc[c][:].bitcast(FP8X4),
                scales=psc[c][:],
                in_=pb[c][:].rearrange("p g n t -> p (g n t)"),
            )

        def attend(c):
            b = coords(c)[0]
            ob[c] = ps("o", 2)
            for jg in range(G):
                n = slice(128 * jg, 128 * (jg + 1))
                nc.tensor.matmul_mx(
                    out=ob[c][:],
                    lhsT=pc[c][:, n].bitcast(FP8X4),
                    lhsT_scale=psc[c][:, n],
                    rhs=vc[b][:, jg, :].bitcast(FP8X4),
                    rhs_scale=vs[b][:, jg, :],
                    start=(jg == 0),
                    stop=(jg == G - 1),
                )

        def silu(c):
            b, ig, t = coords(c)
            pair = wt([P, 2, E], F32, "sl", 3)
            nc.scalar.activation(out=pair[:], in_=u_t[b, ig][:, t : t + 2, :], func=ACT.Silu)
            sl[c] = pair[:, 0, :]
            sl[c + 1] = pair[:, 1, :]

        def gate(c, e0, e1):
            b, ig, t = coords(c)
            k = c // 4
            if t == 0:
                R[k] = wt([P, 4, E], F32, "R", 3)
            nc.vector.scalar_tensor_tensor(
                out=R[k][:, t, e0:e1],
                in0=ob[c][:, e0:e1],
                scalar=1.0 / 32.0,
                in1=sl[c][:, e0:e1],
                op0=ALU.mult,
                op1=ALU.mult,
            )
            nc.sync.dma_start(out=rows(out_0, b, ig)[:, t, e0:e1], in_=R[k][:, t, e0:e1])

        def o_weave(k, part, nparts, eng):
            if k not in obf:
                obf[k] = wt([P, E, 4], BF16, "obf", 2)
            n = E // nparts
            c = slice(n * part, n * (part + 1))
            weave(eng, obf[k][:, c, :], R[k][:, :, c])

        def o_quant(k, part, nparts):
            b, ig = k // G, k % G
            n = E // nparts
            e0 = n * part
            if k not in oc:
                oc[k] = wt([P, E], U32, "oc", 2)
                osc[k] = wt([P, E], U8, "osc", 2)
            c = slice(e0, e0 + n)
            nc.vector.quantize_mx(
                out=oc[k][:, c].bitcast(FP8X4),
                scales=osc[k][:, c],
                in_=obf[k][:, c, :].rearrange("p n t -> p (n t)"),
            )
            m = slice(E * b + e0, E * b + e0 + n)
            nc.sync.dma_start(
                out=out_1[ig, :, m, :].rearrange("p m t -> p (m t)").bitcast(I32),
                in_=oc[k][:, c].bitcast(I32),
            )

        def store_scales(k):
            b, ig = k // G, k % G
            for quad in range(4):
                nc.sync.dma_start(
                    out=out_2[ig, 4 * quad : 4 * quad + 4, E * b : E * (b + 1)].bitcast(I32),
                    in_=osc[k][32 * quad : 32 * quad + 4, :].bitcast(I32),
                )

        transposes(0, 0, 0, "z", 2)
        transposes(0, 0, 1, "z", 2)
        transposes(0, 1, 0, "s", 4)
        transposes(0, 1, 1, "s", 4)
        k_mul(0, 0, 0)
        q_affine(0, 0, 0)
        k_mul(0, 0, 1)
        q_affine(0, 0, 1)
        nc.scalar.mul(out=r_f[:], in_=r_b[:].rearrange("p g t -> p (g t)"), mul=1.0 / D)
        k_mul(0, 1, 0)
        q_weave(0, 0, 0, 2, "V")
        k_quant(0, 0)
        q_quant(0, 0, 0, 2)
        k_mul(0, 1, 1)
        q_affine(0, 1, 0)
        scores(0, 0)
        gain(0, 0)
        k_quant(0, 1)
        scores(0, 1)
        gain(0, 1)
        q_weave(0, 0, 1, 2, "V")
        q_affine(0, 1, 1)
        scores(1, 0)
        scores(1, 1)
        v_weave(0, 0, 0)
        v_weave(0, 0, 1)

        pre = {
            0: [lambda: q_quant(0, 0, 1, 2)],
            1: [lambda: q_weave(0, 1, 0, 2, "V"), lambda: p_quant(0), lambda: q_weave(0, 1, 1, 2, "V")],
            2: [
                lambda: v_quant(0, 0),
                lambda: p_quant(1),
                lambda: q_quant(0, 1, 0, 1),
                lambda: v_quant(0, 1),
                lambda: attend(0),
                lambda: attend(1),
            ],
            3: [lambda: gate(0, 0, E)],
            4: [lambda: k_quant(1, 0)],
            6: [lambda: k_quant(1, 1), lambda: q_quant(1, 0, 0, 1)],
            9: [lambda: v_quant(1, 0), lambda: v_quant(1, 1)],
            10: [lambda: q_quant(1, 1, 0, 2)],
            12: [lambda: q_quant(1, 1, 1, 2), lambda: o_quant(0, 0, 1), lambda: store_scales(0)],
            15: [lambda: o_quant(1, 0, 1), lambda: store_scales(1)],
        }
        post = {
            0: [
                lambda: v_copy(0, 0, 0),
                lambda: v_copy(0, 0, 1),
                lambda: v_weave(0, 1, 0),
                lambda: v_copy(0, 1, 0),
                lambda: v_weave(0, 1, 1),
                lambda: v_copy(0, 1, 1),
            ],
            1: [
                lambda: transposes(1, 0, 0, "z", 2),
            ],
            2: [
                lambda: transposes(1, 0, 1, "z", 2),
                lambda: k_mul(1, 0, 0),
                lambda: q_affine(1, 0, 0),
            ],
            3: [
                lambda: k_mul(1, 0, 1),
                lambda: q_affine(1, 0, 1),
                lambda: transposes(1, 1, 0, "z", 2),
            ],
            4: [
                lambda: transposes(1, 1, 1, "z", 2),
                lambda: k_mul(1, 1, 0),
                lambda: q_weave(1, 0, 0, 2, "V"),
            ],
            5: [
                lambda: q_weave(1, 0, 1, 2, "V"),
                lambda: k_mul(1, 1, 1),
                lambda: q_affine(1, 1, 0),
                lambda: v_weave(1, 0, 0),
            ],
            6: [
                lambda: q_affine(1, 1, 1),
                lambda: v_copy(1, 0, 0),
                lambda: v_weave(1, 0, 1),
                lambda: v_weave(1, 1, 0),
            ],
            7: [
                lambda: v_copy(1, 0, 1),
                lambda: v_copy(1, 1, 0),
                lambda: v_weave(1, 1, 1),
                lambda: q_weave(1, 1, 0, 2, "V"),
            ],
            8: [
                lambda: v_copy(1, 1, 1),
                lambda: o_weave(0, 0, 4, "S"),
                lambda: q_weave(1, 1, 1, 2, "V"),
            ],
            9: [lambda: o_weave(0, 1, 4, "S"), lambda: o_weave(0, 2, 4, "S")],
            10: [lambda: o_weave(0, 3, 4, "S")],
            11: [lambda: o_weave(1, 0, 4, "S")],
            12: [lambda: o_weave(1, 1, 4, "S")],
            13: [lambda: o_weave(1, 2, 4, "S"), lambda: o_weave(1, 3, 4, "S")],
            14: [lambda: o_weave(2, 0, 2, "V"), lambda: o_weave(2, 2, 4, "S")],
            15: [lambda: o_weave(2, 3, 4, "S")],
        }
        for c in range(NCH + 1):
            if c >= 3:
                p_quant(c - 1)
            for f in pre.get(c, []):
                f()
            if c < NCH:
                weights(c, 0)
            if c + 2 < NCH:
                scores(c + 2, 0)
            if c + 1 < NCH:
                gain(c + 1, 0)
            if c >= 3:
                attend(c - 1)
            if c < NCH:
                weights(c, 1)
            if c + 2 < NCH:
                scores(c + 2, 1)
            if c + 1 < NCH:
                gain(c + 1, 1)
            if c % 2 == 1:
                silu(c - 1)
            if c >= 3:
                gate(c - 2, 0, E)
            for f in post.get(c, []):
                f()
        last = NCH - 1
        gate(last, E // 2, E)
        o_weave(3, 1, 2, "S")
        gate(last, 0, E // 2)
        o_quant(2, 0, 1)
        store_scales(2)
        o_weave(3, 0, 2, "V")
        o_quant(3, 1, 2)
        o_quant(3, 0, 2)
        store_scales(3)
